import numpy as np, ml_dtypes
CORES = [113,118,241,246]
N = 4
import mx_ref
BF = ml_dtypes.bfloat16
def entries(a):
    return np.ascontiguousarray(a.T).reshape(-1)
def table(e):
    return np.ascontiguousarray(np.reshape(e, (-1, 16)).T).astype(np.int32)
def cols(t, e):
    v = np.concatenate([t.reshape(128, -1, 4), np.zeros((128, 1, 4), BF)], axis=1)
    return np.ascontiguousarray(v[:, e]).reshape(128, -1)
def tile(rs):
    return np.stack(rs, axis=2).reshape(128, -1).astype(BF)
def cut(t, i, w=512):
    return t[:, w * i:w * i + w]
def f(rng, *shape):
    return mx_ref.flush((rng.standard_normal(shape, dtype=np.float32) * np.exp2(rng.integers(-2, 3, shape[:-1] + (1,)))).astype(BF))
def wide(rng, *shape, cols=0):
    v = rng.standard_normal(shape, dtype=np.float32) * np.exp2(rng.integers(-12, 13, shape)).astype(np.float32)
    if cols: v *= np.repeat(np.exp2(rng.integers(-cols, cols + 1, shape[:-2] + (1, shape[-1] // 4))) * (rng.random(shape[:-2] + (1, shape[-1] // 4)) > 0.0625), 4, axis=-1).astype(np.float32)
    return mx_ref.flush(v.astype(BF))
T, CAPA, CAPB, TR = 512, 160, 136, 40
def mix(rng, n, la=0, lb=0):
    n = n.copy()
    for _ in range(4000):
        p, q = rng.integers(0, N, (2, 3)); k = rng.integers(0, 4)
        p2, q2 = p.copy(), q.copy(); m = n.copy()
        if k == 3: p2[1] = q[1]
        else: p2[k], q2[k] = q[k], p[k]
        m[tuple(p)] -= 1; m[tuple(p2)] += 1
        if k < 3: m[tuple(q)] -= 1; m[tuple(q2)] += 1
        sa, ab = m.sum(axis=2), m.sum(axis=0)
        if m.min() >= 0 and m.max() <= TR and (sa <= CAPA).all() and (sa >= la).all() and (ab <= CAPB).all() and (ab >= lb).all(): n = m
    return n
def even():
    return np.full((N, N, N), T // N ** 2)
def places(rng, k, cap, by=None):
    out = np.zeros(len(k), int)
    for g in np.unique(k):
        j = np.flatnonzero(k == g)
        if by is None: out[j] = g * cap + rng.permutation(cap)[:len(j)]
        else: out[j[np.argsort(by[j])]] = g * cap + cap - 1 - np.arange(len(j))
    return out
def lists(rng, n, back=False):
    s, a, b = np.repeat(np.argwhere(n >= 0), n.reshape(-1), axis=0).T
    col = np.concatenate([rng.permutation(T) for r in range(N)])
    snd, pas, tri = np.full(N * N * CAPA, -1), np.full(N * N * CAPB, -1), np.full(N * N * N * TR, -1)
    p1 = places(rng, s * N + a, CAPA, col if back else None); snd[p1] = col
    arr = s * CAPA + p1 % CAPA
    p2 = places(rng, a * N + b, CAPB, arr if back else None); pas[p2] = arr
    p3 = places(rng, (s * N + a) * N + b, TR, col if back else None); tri[p3] = col
    c, t = a * CAPB + p2 % CAPB, (s * N + a) * TR + p3 % TR
    plc, plt = [], []
    for r in range(N):
        j = rng.permutation(np.flatnonzero(b == r))
        if back: j = j[np.argsort(-c[j])]
        plc.append(table(c[j])); plt.append(table(t[j]))
    return {"snd": np.stack([table(v) for v in snd.reshape(N, -1)]), "pas": np.stack([table(v) for v in pas.reshape(N, -1)]), "tri": np.stack([table(v) for v in tri.reshape(N, -1)]), "plc": np.stack(plc), "plt": np.stack(plt)}
def values(rng):
    return {"x": f(rng, N, 128, 4 * T), "w": f(rng, N, 128, 2048), "vv": f(rng, N, 128, 512)}
def setup_inputs(rng):
    return {**values(rng), **lists(rng, mix(rng, even()))}
def heavy(rng, d):
    n = even()
    for k in range(CAPB // N - T // N ** 2):
        for s in range(N):
            for a in range(N):
                n[s, a, (a + d) % N] += 1; n[s, a, (a + d + 1 + (s + k) % (N - 1)) % N] -= 1
    return {**values(rng), **lists(rng, mix(rng, n, lb=CAPB * np.roll(np.eye(N, dtype=int), d, axis=1)))}
def setup_inputs_diag(rng):
    return heavy(rng, 0)
def setup_inputs_onward(rng):
    return heavy(rng, int(rng.integers(1, N)))
def setup_inputs_full(rng):
    k = T // CAPA
    g = np.zeros((N, N), int); g[:, :k] = CAPA; g[:, k] = T - k * CAPA
    g = np.stack([np.roll(g[s], s) for s in range(N)])[rng.permutation(N)][:, rng.permutation(N)]
    return {**values(rng), **lists(rng, mix(rng, np.repeat(g[:, :, None] // N, N, axis=2), la=np.where(g == CAPA, CAPA, 0)))}
def setup_inputs_reversed(rng):
    return {**values(rng), **lists(rng, mix(rng, even()), back=True)}
def setup_inputs_spread(rng):
    d = setup_inputs(rng); d["x"] = wide(rng, N, 128, 4 * T); return d
def check_inputs(d):
    b = []
    snd, pas, tri, plc, plt = [[entries(d[k][r]) for r in range(N)] for k in ("snd", "pas", "tri", "plc", "plt")]
    for r in range(N):
        if snd[r].min() < -1 or not np.array_equal(np.sort(snd[r][snd[r] >= 0]), np.arange(T)): b.append("snd")
        if tri[r].min() < -1 or not np.array_equal(np.sort(tri[r][tri[r] >= 0]), np.arange(T)): b.append("tri")
        for a in range(N):
            u, v = snd[r][a * CAPA:(a + 1) * CAPA], tri[r][a * N * TR:(a + 1) * N * TR]
            if not np.array_equal(np.sort(u[u >= 0]), np.sort(v[v >= 0])): b.append("tri")
    arrived = [np.concatenate([snd[s][a * CAPA:(a + 1) * CAPA] for s in range(N)]) for a in range(N)]
    for a in range(N):
        if pas[a].min() < -1 or not np.array_equal(np.sort(pas[a][pas[a] >= 0]), np.flatnonzero(arrived[a] >= 0)): b.append("pas")
    if b: return b
    for r in range(N):
        k = np.concatenate([pas[a][r * CAPB:(r + 1) * CAPB] for a in range(N)])
        t = np.concatenate([tri[s][(a * N + r) * TR:(a * N + r + 1) * TR] for s in range(N) for a in range(N)])
        if not np.array_equal(np.sort(plc[r]), np.flatnonzero(k >= 0)): b.append("plc"); continue
        if not np.array_equal(np.sort(plt[r]), np.flatnonzero(t >= 0)): b.append("plt"); continue
        a, m = plc[r] // CAPB, k[plc[r]]
        if (plt[r] // TR != m // CAPA * N + a).any() or (t[plt[r]] != np.stack(arrived)[a, m]).any(): b.append("plt")
    return b
def reference(x, w, vv, snd, pas, tri, plc, plt):
    h = []
    for a in range(N):
        q = mx_ref.quantize(np.concatenate([cols(x[s], entries(snd[s])[a * CAPA:(a + 1) * CAPA]) for s in range(N)], axis=1))
        h.append(tile([np.maximum(mx_ref.matmul(mx_ref.quantize(cut(w[a], i)), q), np.float32(0)) * np.float32(0.043) for i in range(4)]))
    y = np.zeros((N, 128, T), np.float32)
    for b in range(N):
        t = np.concatenate([cols(h[a], entries(pas[a])[b * CAPB:(b + 1) * CAPB]) for a in range(N)], axis=1)
        y[b] = mx_ref.matmul(mx_ref.quantize(vv[b]), mx_ref.quantize(cols(t, entries(plc[b]))))
    return {"y": y}

@@ -1,0 +1,310 @@
+from concourse.bass import DstId, RemoteDMATransfer
+from concourse.mybir import dt, AluOpType, ActivationFunctionType
+
+N, TOK, TR = 4, 512, 40
+BLK = N * TR
+RUN = 2 * TR
+C = 0.043
+
+SCRATCH = {
+    "trib": ("sbuf", [128, N * N * TR // 16], "int32"),
+    "off": ("sbuf", [128, N * N * TR // 16], "uint16"),
+    "xb": ("sbuf", [128, 4 * TOK], "bfloat16"),
+    "xt": ("sbuf", [128, 4 * N * BLK], "bfloat16"),
+    "xq": ("sbuf", [128, N * BLK], "float8_e4m3fn_x4"),
+    "xqs": ("sbuf", [128, N * BLK], "uint8"),
+    "xin": ("sbuf", [128, 3 * BLK], "float8_e4m3fn_x4"),
+    "xins": ("sbuf", [128, 3 * BLK], "uint8"),
+    "wb": ("sbuf", [128, 2048], "bfloat16"),
+    "wq": ("sbuf", [128, 512], "float8_e4m3fn_x4"),
+    "wqs": ("sbuf", [128, 512], "uint8"),
+    "vb": ("sbuf", [128, 512], "bfloat16"),
+    "vq": ("sbuf", [128, 128], "float8_e4m3fn_x4"),
+    "vqs": ("sbuf", [128, 128], "uint8"),
+    "h0": ("sbuf", [128, 8 * BLK], "bfloat16"),
+    "h1": ("sbuf", [128, 8 * BLK], "bfloat16"),
+    "hq0": ("sbuf", [128, BLK], "float8_e4m3fn_x4"),
+    "hqs0": ("sbuf", [128, BLK], "uint8"),
+    "hq1": ("sbuf", [128, BLK], "float8_e4m3fn_x4"),
+    "hqs1": ("sbuf", [128, BLK], "uint8"),
+    "in0": ("sbuf", [128, 5 * RUN], "float8_e4m3fn_x4"),
+    "ins0": ("sbuf", [128, 5 * RUN], "uint8"),
+    "in1": ("sbuf", [128, 5 * RUN], "float8_e4m3fn_x4"),
+    "ins1": ("sbuf", [128, 5 * RUN], "uint8"),
+    "pltb": ("sbuf", [128, TOK // 16], "int32"),
+    "off2": ("sbuf", [128, TOK // 16], "uint16"),
+    "r": ("sbuf", [128, N * BLK], "float32"),
+    "yb": ("sbuf", [128, TOK], "float32"),
+    "psp": ("psum", [128, 2048], "float32"),
+    "psq": ("psum", [128, 2048], "float32"),
+}
+TEMPS = ["t1", "u", "q", "s", "ai", "si", "hs", "ha", "ph", "f", "g2", "d", "d2", "g1", "g3"]
+for _n in TEMPS:
+    SCRATCH["tmp_" + _n] = ("sbuf", [128, TOK // 16], "int32")
+
+SEMAPHORES = ["ltri", "lx", "lw", "lvv", "lplt", "off", "qw", "qv", "ar", "off2", "yv", "ys", "yst", "sent",
+              "xn", "xa", "xf", "cs", "cv"]
+for _k in "ABNO":
+    SEMAPHORES += ["gv" + _k, "gs" + _k, "q" + _k, "rv" + _k, "rs" + _k]
+    SEMAPHORES += ["m%s%d" % (_k, _i) for _i in range(4)]
+SEMAPHORES += ["rvG", "rsG", "q0F", "q0G", "q1F", "q1G", "h0N", "h0F", "h1N", "h1F", "v0N", "v0F", "v1N", "v1F"]
+
+
+def rank_program(g, core, T, topo):
+    me = T.rank_of(core)
+    if me is None:
+        return
+    S = T.sem
+    vec, act, ten, syn = g.vector, g.scalar, g.tensor, g.sync
+    A = AluOpType
+    F = ActivationFunctionType
+
+    def chip_ranks(c):
+        return [r for r in range(N) if T.cores[r] in topo.cores_of(c)]
+
+    grp = chip_ranks(core)
+    far = [r for r in range(N) if r not in grp]
+    if len(grp) != 2 or grp[0] % 2 or grp[1] != grp[0] + 1 or chip_ranks(T.cores[far[0]]) != far:
+        raise ValueError("the ranks must lie in neighbouring pairs on two chips")
+    idx = grp.index(me)
+    near = grp[1 - idx]
+    gme = grp[0] // 2
+    order = {"A": far[idx], "B": far[1 - idx], "N": near, "O": me}
+
+    fe = topo.engines(core, T.cores[far[0]])
+    ne = [e for e in topo.engines(core, T.cores[near]) if e not in fe]
+
+    def bits(es):
+        return sum(1 << e for e in es)
+
+    FULL, LOW, HIGH, NEAR = bits(fe), bits(fe[:len(fe) // 2]), bits(fe[len(fe) // 2:]), bits(ne)
+    nsent = [0]
+
+    def count(m):
+        return bin(m).count("1")
+
+    def did(r):
+        rid, pid = topo.addr(T.cores[r], core)
+        return DstId(rid=rid, pnc=pid)
+
+    def send(dst, out, in_, sem, mask):
+        rid, pid = topo.addr(T.cores[dst], core)
+        g.remote_dma(out, in_, S[sem], S.sent, pid, rid, mask)
+        nsent[0] += count(mask)
+
+    def fused(items):
+        tr = [RemoteDMATransfer(dst_ids=[did(dst)], dma_engine_mask=mask, remote_sem=S[sem], src=in_, dst=out)
+              for dst, out, in_, sem, mask in items]
+        g.remote_dma_fused(tr, local_sem=S.sent)
+        nsent[0] += sum(count(it[4]) for it in items)
+
+    def codes(b, lo, n):
+        return T[b][:, lo:lo + n].bitcast(dt.uint8)
+
+    def plane(b, lo, n):
+        return T[b][:, lo:lo + n]
+
+    for k in range(4):
+        syn.dma_start(T.trib[16 * k:16 * k + 16, :], T.tri[:]).then_inc(S.ltri, 16)
+        act.dma_start(T.trib[16 * (k + 4):16 * (k + 4) + 16, :], T.tri[:]).then_inc(S.ltri, 16)
+    syn.dma_start(T.xb[:], T.x[:]).then_inc(S.lx, 16)
+    syn.dma_start(T.wb[:], T.w[:]).then_inc(S.lw, 16)
+    syn.dma_start(T.vb[:], T.vv[:]).then_inc(S.lvv, 16)
+    for k in range(8):
+        syn.dma_start(T.pltb[16 * k:16 * k + 16, :], T.plt[:]).then_inc(S.lplt, 16)
+
+    vec.wait_ge(S.ltri, 128)
+    vec.tensor_scalar(T.off[:], T.trib[:], 4, 0, A.mult, A.max).then_inc(S.off, 1)
+    vec.wait_ge(S.off, 1)
+    vec.wait_ge(S.lx, 16)
+    act.wait_ge(S.off, 1)
+    act.wait_ge(S.lx, 16)
+    KO = BLK // 16
+    for k in "ABNO":
+        a = order[k]
+        o = T.off[:, KO * a:KO * a + KO]
+        for t in range(4):
+            out = T.xt[:, 4 * BLK * a + t:4 * BLK * (a + 1):4]
+            win = T.xb[:, t:4 * TOK].indirect(o)
+            if t < 2:
+                vec.tensor_copy(out, win).then_inc(S["gv" + k], 1)
+            else:
+                act.activation(out, win, F.Copy).then_inc(S["gs" + k], 1)
+        vec.wait_ge(S["gv" + k], 2)
+        vec.wait_ge(S["gs" + k], 2)
+        vec.quantize_mx(T.xq[:, BLK * a:BLK * (a + 1)], T.xqs[:, BLK * a:BLK * (a + 1)],
+                        T.xt[:, 4 * BLK * a:4 * BLK * (a + 1)]).then_inc(S["q" + k], 1)
+
+    for k in "ABN":
+        d = order[k]
+        lo = 0 if k == "N" else BLK * (1 + idx)
+        sem = {"N": "xn"}.get(k) or ("xa" if k == "A" else "xf")
+        mask = NEAR if k == "N" else FULL
+        g.wait_ge(S["q" + k], 1)
+        send(d, codes("xin", lo, BLK), codes("xq", BLK * d, BLK), sem, mask)
+        send(d, plane("xins", lo, BLK), plane("xqs", BLK * d, BLK), sem, mask)
+
+    vec.wait_ge(S.lw, 16)
+    vec.quantize_mx(T.wq[:], T.wqs[:], T.wb[:]).then_inc(S.qw, 1)
+
+    def products(k, ps, buf, sbuf, lo):
+        for i in range(4):
+            ten.matmul_mx(T[ps][:, 512 * i:512 * i + BLK], T.wq[:, 128 * i:128 * i + 128], T.wqs[:, 128 * i:128 * i + 128],
+                          T[buf][:, lo:lo + BLK], T[sbuf][:, lo:lo + BLK], True, True).then_inc(S["m%s%d" % (k, i)], 1)
+
+    def relu(i, ps, h, si, b0, nb, tail):
+        src = T[ps][:, 512 * i + TR * b0:512 * i + TR * (b0 + nb)]
+        out = T[h][:, 8 * TR * b0 + 4 * si + i:8 * TR * (b0 + nb):8]
+        if i % 2:
+            vec.tensor_scalar(out, src, 0.0, C, A.max, A.mult).then_inc(S["rv" + tail], 1)
+        else:
+            act.activation(out, src, F.Relu, scale=C).then_inc(S["rs" + tail], 1)
+
+    def await_bank(k, i):
+        (vec if i % 2 else act).wait_ge(S["m%s%d" % (k, i)], 1)
+
+    far_b, grp_b = far[0], grp[0]
+    pair = 240 if idx == 0 else 0
+
+    def quant(p, which):
+        b0 = far_b if which == "F" else grp_b
+        src = T["h%d" % p][:, 8 * TR * b0:8 * TR * (b0 + 2)]
+        if which == "F":
+            vec.quantize_mx(T["hq%d" % p][:], T["hqs%d" % p][:], src).then_inc(S["q%dF" % p], 1)
+        else:
+            vec.quantize_mx(T["in%d" % p][:, pair:pair + BLK], T["ins%d" % p][:, pair:pair + BLK], src).then_inc(S["q%dG" % p], 1)
+
+    def far_place(d):
+        return (0 if far.index(d) == 0 else 240) + RUN * (1 - idx)
+
+    mate_out = pair + RUN * (1 - idx)
+
+    def far_items(p, view, src, dst, m):
+        return [(d, view("%s%d" % (dst, p), far_place(d), RUN), view("%s%d" % (src, p), RUN * j, RUN), "h%dF" % p, m[j])
+                for j, d in enumerate(far)]
+
+    def near_item(p, view, buf):
+        return (near, view("%s%d" % (buf, p), 160, RUN), view("%s%d" % (buf, p), mate_out, RUN), "h%dN" % p, NEAR)
+
+    ten.wait_ge(S.qw, 1)
+    ten.wait_ge(S.qO, 1)
+    products("O", "psp", "xq", "xqs", BLK * me)
+    ten.wait_ge(S.xn, 2 * len(ne))
+    products("N", "psq", "xin", "xins", 0)
+    for i in range(4):
+        await_bank("O", i)
+        relu(i, "psp", "h0", idx, 0, 4, "O")
+    vec.wait_ge(S.lvv, 16)
+    vec.quantize_mx(T.vq[:], T.vqs[:], T.vb[:]).then_inc(S.qv, 1)
+    for i in range(4):
+        await_bank("N", i)
+        relu(i, "psq", "h0", 1 - idx, 0, 4, "N")
+    for k in "ON":
+        vec.wait_ge(S["rv" + k], 2)
+        vec.wait_ge(S["rs" + k], 2)
+    quant(0, "F")
+    quant(0, "G")
+    g.wait_ge(S.q0F, 1)
+    g.wait_ge(S.q0G, 1)
+    fused(far_items(0, codes, "hq", "in", (LOW, HIGH)) + [near_item(0, codes, "in")])
+    fused(far_items(0, plane, "hqs", "ins", (LOW, HIGH)) + [near_item(0, plane, "ins")])
+
+    ten.wait_ge(S.xa, 2 * len(fe))
+    for k in ("rvO", "rsO"):
+        ten.wait_ge(S[k], 2)
+    products("A", "psp", "xin", "xins", BLK * (1 + idx))
+    ten.wait_ge(S.xf, 2 * len(fe))
+    for k in ("rvN", "rsN"):
+        ten.wait_ge(S[k], 2)
+    products("B", "psq", "xin", "xins", BLK * (2 - idx))
+    for i in range(4):
+        await_bank("A", i)
+        relu(i, "psp", "h1", idx, 0, 4, "A")
+    for i in range(4):
+        await_bank("B", i)
+        relu(i, "psq", "h1", 1 - idx, far_b, 2, "B")
+        if i < 2:
+            relu(i, "psq", "h1", 1 - idx, grp_b, 2, "G")
+    vec.wait_ge(S.rvA, 2)
+    vec.wait_ge(S.rsA, 2)
+    vec.wait_ge(S.rvB, 2)
+    vec.wait_ge(S.rsB, 2)
+    quant(1, "F")
+    for i in (2, 3):
+        relu(i, "psq", "h1", 1 - idx, grp_b, 2, "G")
+    vec.wait_ge(S.rvG, 2)
+    vec.wait_ge(S.rsG, 2)
+    quant(1, "G")
+    g.wait_ge(S.q1F, 1)
+    fused(far_items(1, codes, "hq", "in", (LOW, HIGH)))
+    fused(far_items(1, plane, "hqs", "ins", (LOW, HIGH)))
+    g.wait_ge(S.q1G, 1)
+    it = near_item(1, codes, "in")
+    send(*it)
+    it = near_item(1, plane, "ins")
+    send(*it)
+
+    n = [0]
+
+    def level(*calls):
+        for c in calls:
+            c.then_inc(S.ar, 1)
+            n[0] += 1
+        vec.wait_ge(S.ar, n[0])
+
+    def ts(o, i, s1, s2, op0, op1=None):
+        if op1 is None:
+            return vec.tensor_scalar(T["tmp_" + o][:], i, s1, None, op0)
+        return vec.tensor_scalar(T["tmp_" + o][:], i, s1, s2, op0, op1)
+
+    def tt(o, a, b, op):
+        return vec.tensor_tensor(T["tmp_" + o][:], T["tmp_" + a][:], T["tmp_" + b][:], op)
+
+    vec.wait_ge(S.lplt, 128)
+    q = T.tmp_q[:]
+    SH = A.arith_shift_right
+    AND = A.bitwise_and
+    level(ts("t1", T.pltb[:], 1639, None, A.mult), ts("u", T.pltb[:], 2, None, A.mult))
+    level(ts("q", T.tmp_t1[:], 16, None, SH))
+    level(ts("s", q, 2, None, SH), ts("ai", q, 1, None, AND), ts("si", q, 2, 1, SH, AND),
+          ts("hs", q, 3, None, SH), ts("ha", q, 1, 1, SH, AND))
+    level(tt("ph", "hs", "ha", A.not_equal), ts("f", T.tmp_ai[:], -160, 80, A.mult, A.add), tt("g2", "u", "si", A.add))
+    level(tt("d", "ph", "s", A.subtract), tt("g1", "f", "g2", A.add))
+    level(ts("d2", T.tmp_d[:], 320, None, A.mult))
+    level(tt("g3", "g1", "d2", A.add))
+    vec.tensor_copy(T.off2[:], T.tmp_g3[:]).then_inc(S.off2, 1)
+
+    ten.wait_ge(S.qv, 1)
+    for k in ("rvA", "rsA"):
+        ten.wait_ge(S[k], 2)
+    local_lo, far_lo = (160, 0) if idx == 0 else (80, 240)
+    for j, (p, w) in enumerate(((0, "N"), (0, "F"), (1, "N"), (1, "F"))):
+        if w == "N":
+            ten.wait_ge(S["q%dG" % p], 1)
+            ten.wait_ge(S["h%dN" % p], 2 * len(ne))
+        else:
+            ten.wait_ge(S["h%dF" % p], 2 * len(fe))
+        lo = local_lo if w == "N" else far_lo
+        ten.matmul_mx(T.psp[:, 512 * j:512 * j + BLK], T.vq[:], T.vqs[:],
+                      T["in%d" % p][:, lo:lo + BLK], T["ins%d" % p][:, lo:lo + BLK], True, True).then_inc(S["v%d%s" % (p, w)], 1)
+        place = 320 * p + 160 * (gme if w == "N" else 1 - gme)
+        out, src = T.r[:, place:place + BLK], T.psp[:, 512 * j:512 * j + BLK]
+        if j < 3:
+            act.wait_ge(S["v%d%s" % (p, w)], 1)
+            act.activation(out, src, F.Copy).then_inc(S.cs, 1)
+        else:
+            vec.wait_ge(S["v%d%s" % (p, w)], 1)
+            vec.tensor_copy(out, src).then_inc(S.cv, 1)
+
+    H = TOK // 2
+    for q_, lo in ((vec, 0), (act, H)):
+        q_.wait_ge(S.off2, 1)
+        q_.wait_ge(S.cs, 3)
+        q_.wait_ge(S.cv, 1)
+    vec.tensor_copy(T.yb[:, :H], T.r[:].indirect(T.off2[:, :H // 16])).then_inc(S.yv, 1)
+    act.activation(T.yb[:, H:], T.r[:].indirect(T.off2[:, H // 16:]), F.Copy).then_inc(S.ys, 1)
+    syn.wait_ge(S.yv, 1)
+    syn.wait_ge(S.ys, 1)
+    syn.dma_start(T.y[:], T.yb[:]).then_inc(S.yst, 16)
+    syn.wait_ge(S.yst, 16)
+    g.wait_ge(S.sent, nsent[0])

@@ -4,6 +4,8 @@ from concourse.mybir import dt, AluOpType, ActivationFunctionType
 N, TOK, TR = 4, 512, 40
 BLK = N * TR
 RUN = 2 * TR
+WIN = 128
+HALF = 2 * BLK + 1
 C = 0.043
 
 SCRATCH = {
@@ -11,10 +13,10 @@ SCRATCH = {
     "off": ("sbuf", [128, N * N * TR // 16], "uint16"),
     "xb": ("sbuf", [128, 4 * TOK], "bfloat16"),
     "xt": ("sbuf", [128, 4 * N * BLK], "bfloat16"),
-    "xq": ("sbuf", [128, N * BLK], "float8_e4m3fn_x4"),
-    "xqs": ("sbuf", [128, N * BLK], "uint8"),
-    "xin": ("sbuf", [128, 3 * BLK], "float8_e4m3fn_x4"),
-    "xins": ("sbuf", [128, 3 * BLK], "uint8"),
+    "xq": ("sbuf", [128, (N + 2) * BLK], "float8_e4m3fn_x4"),
+    "xqs": ("sbuf", [128, (N + 2) * BLK], "uint8"),
+    "xin": ("sbuf", [128, 2 * BLK], "float8_e4m3fn_x4"),
+    "xins": ("sbuf", [128, 2 * BLK], "uint8"),
     "wb": ("sbuf", [128, 2048], "bfloat16"),
     "wq": ("sbuf", [128, 512], "float8_e4m3fn_x4"),
     "wqs": ("sbuf", [128, 512], "uint8"),
@@ -33,21 +35,29 @@ SCRATCH = {
     "ins1": ("sbuf", [128, 5 * RUN], "uint8"),
     "pltb": ("sbuf", [128, TOK // 16], "int32"),
     "off2": ("sbuf", [128, TOK // 16], "uint16"),
-    "r": ("sbuf", [128, N * BLK], "float32"),
+    "r": ("sbuf", [128, 2 * HALF - 1], "float32"),
     "yb": ("sbuf", [128, TOK], "float32"),
     "psp": ("psum", [128, 2048], "float32"),
     "psq": ("psum", [128, 2048], "float32"),
 }
-TEMPS = ["t1", "u", "q", "s", "ai", "si", "hs", "ha", "ph", "f", "g2", "d", "d2", "g1", "g3"]
-for _n in TEMPS:
+for _n in ("u", "a", "b", "c", "d"):
     SCRATCH["tmp_" + _n] = ("sbuf", [128, TOK // 16], "int32")
 
-SEMAPHORES = ["ltri", "lx", "lw", "lvv", "lplt", "off", "qw", "qv", "ar", "off2", "yv", "ys", "yst", "sent",
-              "xn", "xa", "xf", "cs", "cv"]
-for _k in "ABNO":
-    SEMAPHORES += ["gv" + _k, "gs" + _k, "q" + _k, "rv" + _k, "rs" + _k]
+SEMAPHORES = ["ltri", "lx", "lw", "lvv", "lplt", "off", "qw", "qv", "ar1", "ar2", "ar3", "off2", "cp", "y0", "y1", "yst", "sent"]
+for _k in "ADNO":
+    SEMAPHORES += ["g" + _k, "q" + _k]
+for _k in "OANBCMK":
+    SEMAPHORES += ["x" + _k]
+    SEMAPHORES += ["r%s%s%s" % (_k, _q, _p) for _q in "VS" for _p in ("", "F", "G")]
     SEMAPHORES += ["m%s%d" % (_k, _i) for _i in range(4)]
-SEMAPHORES += ["rvG", "rsG", "q0F", "q0G", "q1F", "q1G", "h0N", "h0F", "h1N", "h1F", "v0N", "v0F", "v1N", "v1F"]
+SEMAPHORES += ["q0F", "q0G", "q1F", "q1G", "h0N", "h0F", "h1N", "h1F", "v0N", "v0F", "v1N", "v1F"]
+
+OPT = dict(
+    V="off gA0 gA1 qA gN0 gN3 qN gD3 qD qw gO3 qO rO1 rO3 rN1 rN3 q0F rA1 q0G rB1 rB3 q1F rC1 rC3 q1G qv plt c1F y0 y1",
+    S="gA2 gA3 gN1 gN2 gD0 gD1 gD2 gO0 gO1 gO2 rO0 rO2 rN0 rN2 rA0 rA2 rA3 rB0 rB2 rC0 rC2 c0F c0N c1N y0 y1",
+    G="Ac Nc As+Ns Ds Bc Cc 0Fc 0Fs 1Fc+0Nc 1Fs+0Ns 1Nc 1Ns",
+    T="O N A B C 0F 0N 1N 1F",
+)
 
 
 def rank_program(g, core, T, topo):
@@ -58,6 +68,7 @@ def rank_program(g, core, T, topo):
     vec, act, ten, syn = g.vector, g.scalar, g.tensor, g.sync
     A = AluOpType
     F = ActivationFunctionType
+    orders = {k: v.split() for k, v in OPT.items()}
 
     def chip_ranks(c):
         return [r for r in range(N) if T.cores[r] in topo.cores_of(c)]
@@ -69,7 +80,7 @@ def rank_program(g, core, T, topo):
     idx = grp.index(me)
     near = grp[1 - idx]
     gme = grp[0] // 2
-    order = {"A": far[idx], "B": far[1 - idx], "N": near, "O": me}
+    block = {"A": far[idx], "D": far[1 - idx], "N": near, "O": me}
 
     fe = topo.engines(core, T.cores[far[0]])
     ne = [e for e in topo.engines(core, T.cores[near]) if e not in fe]
@@ -77,234 +88,217 @@ def rank_program(g, core, T, topo):
     def bits(es):
         return sum(1 << e for e in es)
 
-    FULL, LOW, HIGH, NEAR = bits(fe), bits(fe[:len(fe) // 2]), bits(fe[len(fe) // 2:]), bits(ne)
-    nsent = [0]
+    def halves(es):
+        return bits(es[:len(es) // 2]), bits(es[len(es) // 2:])
 
-    def count(m):
-        return bin(m).count("1")
+    FULL, NEAR = bits(fe), bits(ne)
 
-    def did(r):
-        rid, pid = topo.addr(T.cores[r], core)
-        return DstId(rid=rid, pnc=pid)
+    full = {"ltri": 32, "lx": 16, "lw": 16, "lvv": 16, "lplt": 32, "off": 4, "ar1": 3, "off2": 4, "cp": 7, "y0": 2, "y1": 2}
+    for k in "ADNO":
+        full["g" + k] = 4
+    relu_sem = {}
+    for qn in "VS":
+        for w in orders[qn]:
+            if w[0] == "r":
+                relu_sem[w] = w[:2] + qn + w[3:]
+                full[relu_sem[w]] = full.get(relu_sem[w], 0) + 1
+    seen = set()
 
-    def send(dst, out, in_, sem, mask):
-        rid, pid = topo.addr(T.cores[dst], core)
-        g.remote_dma(out, in_, S[sem], S.sent, pid, rid, mask)
-        nsent[0] += count(mask)
+    def wait(qn, q, *sems):
+        for s in sems:
+            if (qn, s) not in seen:
+                seen.add((qn, s))
+                q.wait_ge(S[s], full.get(s, 1))
 
-    def fused(items):
-        tr = [RemoteDMATransfer(dst_ids=[did(dst)], dma_engine_mask=mask, remote_sem=S[sem], src=in_, dst=out)
-              for dst, out, in_, sem, mask in items]
-        g.remote_dma_fused(tr, local_sem=S.sent)
-        nsent[0] += sum(count(it[4]) for it in items)
+    def relus(ks, banks, parts):
+        return [s for w, s in relu_sem.items() if w[1] in ks and w[2] in banks and w[3:] in parts]
 
-    def codes(b, lo, n):
-        return T[b][:, lo:lo + n].bitcast(dt.uint8)
-
-    def plane(b, lo, n):
-        return T[b][:, lo:lo + n]
-
-    for k in range(4):
-        syn.dma_start(T.trib[16 * k:16 * k + 16, :], T.tri[:]).then_inc(S.ltri, 16)
-        act.dma_start(T.trib[16 * (k + 4):16 * (k + 4) + 16, :], T.tri[:]).then_inc(S.ltri, 16)
+    syn.dma_start(T.trib[0:16, :], T.tri[:]).then_inc(S.ltri, 16)
+    act.dma_start(T.trib[16:32, :], T.tri[:]).then_inc(S.ltri, 16)
     syn.dma_start(T.xb[:], T.x[:]).then_inc(S.lx, 16)
     syn.dma_start(T.wb[:], T.w[:]).then_inc(S.lw, 16)
     syn.dma_start(T.vb[:], T.vv[:]).then_inc(S.lvv, 16)
-    for k in range(8):
+    for k in range(2):
         syn.dma_start(T.pltb[16 * k:16 * k + 16, :], T.plt[:]).then_inc(S.lplt, 16)
 
-    vec.wait_ge(S.ltri, 128)
-    vec.tensor_scalar(T.off[:], T.trib[:], 4, 0, A.mult, A.max).then_inc(S.off, 1)
-    vec.wait_ge(S.off, 1)
-    vec.wait_ge(S.lx, 16)
-    act.wait_ge(S.off, 1)
-    act.wait_ge(S.lx, 16)
-    KO = BLK // 16
-    for k in "ABNO":
-        a = order[k]
-        o = T.off[:, KO * a:KO * a + KO]
-        for t in range(4):
-            out = T.xt[:, 4 * BLK * a + t:4 * BLK * (a + 1):4]
-            win = T.xb[:, t:4 * TOK].indirect(o)
-            if t < 2:
-                vec.tensor_copy(out, win).then_inc(S["gv" + k], 1)
-            else:
-                act.activation(out, win, F.Copy).then_inc(S["gs" + k], 1)
-        vec.wait_ge(S["gv" + k], 2)
-        vec.wait_ge(S["gs" + k], 2)
-        vec.quantize_mx(T.xq[:, BLK * a:BLK * (a + 1)], T.xqs[:, BLK * a:BLK * (a + 1)],
-                        T.xt[:, 4 * BLK * a:4 * BLK * (a + 1)]).then_inc(S["q" + k], 1)
-
-    for k in "ABN":
-        d = order[k]
-        lo = 0 if k == "N" else BLK * (1 + idx)
-        sem = {"N": "xn"}.get(k) or ("xa" if k == "A" else "xf")
-        mask = NEAR if k == "N" else FULL
-        g.wait_ge(S["q" + k], 1)
-        send(d, codes("xin", lo, BLK), codes("xq", BLK * d, BLK), sem, mask)
-        send(d, plane("xins", lo, BLK), plane("xqs", BLK * d, BLK), sem, mask)
-
-    vec.wait_ge(S.lw, 16)
-    vec.quantize_mx(T.wq[:], T.wqs[:], T.wb[:]).then_inc(S.qw, 1)
-
-    def products(k, ps, buf, sbuf, lo):
-        for i in range(4):
-            ten.matmul_mx(T[ps][:, 512 * i:512 * i + BLK], T.wq[:, 128 * i:128 * i + 128], T.wqs[:, 128 * i:128 * i + 128],
-                          T[buf][:, lo:lo + BLK], T[sbuf][:, lo:lo + BLK], True, True).then_inc(S["m%s%d" % (k, i)], 1)
-
-    def relu(i, ps, h, si, b0, nb, tail):
-        src = T[ps][:, 512 * i + TR * b0:512 * i + TR * (b0 + nb)]
-        out = T[h][:, 8 * TR * b0 + 4 * si + i:8 * TR * (b0 + nb):8]
-        if i % 2:
-            vec.tensor_scalar(out, src, 0.0, C, A.max, A.mult).then_inc(S["rv" + tail], 1)
-        else:
-            act.activation(out, src, F.Relu, scale=C).then_inc(S["rs" + tail], 1)
-
-    def await_bank(k, i):
-        (vec if i % 2 else act).wait_ge(S["m%s%d" % (k, i)], 1)
-
     far_b, grp_b = far[0], grp[0]
-    pair = 240 if idx == 0 else 0
+    pair = 3 * RUN if idx == 0 else 0
+    local_lo, far_lo = (2 * RUN, 0) if idx == 0 else (RUN, 3 * RUN)
 
-    def quant(p, which):
-        b0 = far_b if which == "F" else grp_b
-        src = T["h%d" % p][:, 8 * TR * b0:8 * TR * (b0 + 2)]
-        if which == "F":
-            vec.quantize_mx(T["hq%d" % p][:], T["hqs%d" % p][:], src).then_inc(S["q%dF" % p], 1)
+    def mine(r):
+        return BLK * (1 + r)
+
+    n_at = (N + 1) * BLK * gme
+
+    def far_at(sender_chip):
+        return {"A": BLK * sender_chip, "D": BLK * (1 - sender_chip)}
+
+    def pieces(k):
+        if k in "NMK":
+            lo, n = {"N": (0, BLK), "M": (RUN * (1 - gme), RUN), "K": (RUN * gme, RUN)}[k]
+            return [(near, "xq", n_at + lo, "xq", mine(near) + lo, n, NEAR, {"N": "xM"}.get(k, "x" + k), "qN")]
+        if k == "A":
+            return [(block[k], "xin", far_at(gme)[k], "xq", mine(block[k]), BLK, FULL, "xA", "qA")]
+        if k in "DBC":
+            lo, n = {"D": (0, BLK), "B": (RUN * gme, RUN), "C": (RUN * (1 - gme), RUN)}[k]
+            return [(block["D"], "xin", far_at(gme)["D"] + lo, "xq", mine(block["D"]) + lo, n, FULL, {"D": "xB"}.get(k, "x" + k), "qD")]
+        p = k[0]
+        if k[1] == "N":
+            return [(near, "in" + p, 2 * RUN, "in" + p, pair + RUN * (1 - idx), RUN, NEAR, "h" + k, "q%sG" % p)]
+        return [(d, "in" + p, 3 * RUN * j + RUN * idx, "hq" + p, RUN * j, RUN, FULL, "h" + k, "q" + k) for j, d in enumerate(far)]
+
+    calls = []
+    for call in orders["G"]:
+        ps = [list(p) + [it[-1]] for it in call.split("+") for p in pieces(it[:-1])]
+        for mask, es in ((FULL, fe), (NEAR, ne)):
+            two = [p for p in ps if p[6] == mask]
+            if len(two) == 2:
+                two[0][6], two[1][6] = halves(es)
+        calls.append(ps)
+        for p in ps:
+            for k in (p[7], "sent"):
+                full[k] = full.get(k, 0) + bin(p[6]).count("1")
+    at = far_at(1 - gme)
+    skip = (WIN - RUN) * gme
+    first, second = RUN * (1 - gme) - skip, RUN * gme - skip
+    window = {"O": ("xq", mine(me), BLK), "A": ("xin", at["A"], BLK), "N": ("xq", n_at, BLK),
+              "M": ("xq", n_at + first, WIN), "K": ("xq", n_at + second, WIN),
+              "B": ("xin", at["D"] + first, WIN), "C": ("xin", at["D"] + second, WIN)}
+    needs = {"O": ["qO"], "N": ["xM"], "A": ["xA"], "M": ["qN", "qO", "xM"], "K": ["xM", "xK"], "B": ["xA", "xB"], "C": ["xB", "xC"]}
+
+    wjob = [w for w in orders["T"] if len(w) == 1]
+    vjob = [w for w in orders["T"] if len(w) == 2]
+    yjob = [w for w in orders["V"] if w[0] == "y"]
+    bank = {w: ("psp", "psq")[j % 2] for j, w in enumerate(wjob)}
+    vbank = bank[wjob[-2]]
+    KO = BLK // 16
+
+    def do(qn, q, w):
+        def copy(out, src):
+            return q.tensor_copy(out, src) if qn == "V" else q.activation(out, src, F.Copy)
+
+        if w == "off":
+            wait(qn, q, "ltri")
+            for p in range(0, 128, 32):
+                q.tensor_scalar(T.off[p:p + 32, :], T.trib[0:32, :], 4, 0, A.mult, A.max).then_inc(S.off, 1)
+        elif w == "qw":
+            wait(qn, q, "lw")
+            q.quantize_mx(T.wq[:], T.wqs[:], T.wb[:]).then_inc(S.qw, 1)
+        elif w == "qv":
+            wait(qn, q, "lvv")
+            q.quantize_mx(T.vq[:], T.vqs[:], T.vb[:]).then_inc(S.qv, 1)
+        elif w == "plt":
+            e = T.pltb[0:32, :]
+            t = {k: T["tmp_" + k][0:32, :] for k in "uabcd"}
+            wait(qn, q, "lplt")
+            q.memset(T.r[:, HALF - 1:HALF], 0.0).then_inc(S.cp, 1)
+            q.tensor_scalar(t["u"], e, 2, None, A.mult).then_inc(S.ar1, 1)
+            q.tensor_scalar(t["a"], e, BLK, 2 - HALF, A.is_ge, A.mult).then_inc(S.ar1, 1)
+            q.tensor_scalar(t["b"], e, 3 * BLK, 2 - HALF, A.is_ge, A.mult).then_inc(S.ar1, 1)
+            wait(qn, q, "ar1")
+            q.tensor_tensor(t["c"], t["u"], t["a"], A.add).then_inc(S.ar2, 1)
+            wait(qn, q, "ar2")
+            q.tensor_tensor(t["d"], t["c"], t["b"], A.add).then_inc(S.ar3, 1)
+            wait(qn, q, "ar3")
+            for p in range(0, 128, 32):
+                q.tensor_copy(T.off2[p:p + 32, :], t["d"]).then_inc(S.off2, 1)
+        elif w[0] == "y":
+            n = TOK // (2 * len(yjob))
+            lo = n * (2 * int(w[1]) + (qn == "S"))
+            wait(qn, q, "off2", "cp")
+            copy(T.yb[:, lo:lo + n], T.r[:].indirect(T.off2[:, lo // 16:(lo + n) // 16])).then_inc(S[w], 1)
+        elif w[0] == "g":
+            a, t = block[w[1]], int(w[2])
+            wait(qn, q, "off", "lx")
+            copy(T.xt[:, 4 * BLK * a + t:4 * BLK * (a + 1):4],
+                 T.xb[:, t:4 * TOK].indirect(T.off[:, KO * a:KO * a + KO])).then_inc(S["g" + w[1]], 1)
+        elif w[0] == "q" and len(w) == 2:
+            a = block[w[1]]
+            wait(qn, q, "g" + w[1])
+            q.quantize_mx(T.xq[:, mine(a):mine(a) + BLK], T.xqs[:, mine(a):mine(a) + BLK],
+                          T.xt[:, 4 * BLK * a:4 * BLK * (a + 1)]).then_inc(S[w], 1)
+        elif w[0] == "r":
+            k, i = w[1], int(w[2])
+            part = "F" if k in "MB" else "G" if k in "KC" else w[3:]
+            b0, nb = {"": (0, 4), "F": (far_b, 2), "G": (grp_b, 2)}[part]
+            si = idx if k in "OA" else 1 - idx
+            lo = 512 * i + (TR * b0 if k in "OAN" else skip)
+            src = T[bank[k]][:, lo:lo + TR * nb]
+            out = T["h0" if k in "ONMK" else "h1"][:, 8 * TR * b0 + 4 * si + i:8 * TR * (b0 + nb):8]
+            wait(qn, q, "m%s%d" % (k, i))
+            if qn == "V":
+                q.tensor_scalar(out, src, 0.0, C, A.max, A.mult).then_inc(S[relu_sem[w]], 1)
+            else:
+                q.activation(out, src, F.Relu, scale=C).then_inc(S[relu_sem[w]], 1)
+        elif w[0] == "q":
+            p, part = w[1], w[2]
+            b0 = far_b if part == "F" else grp_b
+            src = T["h" + p][:, 8 * TR * b0:8 * TR * (b0 + 2)]
+            wait(qn, q, *relus({"0F": "ONM", "0G": "ONK", "1F": "AB", "1G": "AC"}[w[1:]], "0123", ("", part)))
+            if part == "F":
+                q.quantize_mx(T["hq" + p][:], T["hqs" + p][:], src).then_inc(S[w], 1)
+            else:
+                q.quantize_mx(T["in" + p][:, pair:pair + BLK], T["ins" + p][:, pair:pair + BLK], src).then_inc(S[w], 1)
+        elif w[0] == "c":
+            j = vjob.index(w[1:])
+            ga = gme if w[2] == "N" else 1 - gme
+            gs = ga if w[1] == "0" else 1 - ga
+            place = HALF * gs + BLK * ga
+            ps = T[vbank]
+            wait(qn, q, "v" + w[1:])
+            if w[2] == "F":
+                copy(T.r[:, place:place + BLK], ps[:, 512 * j:512 * j + BLK]).then_inc(S.cp, 1)
+            else:
+                copy(T.r[:, place:place + RUN], ps[:, 512 * j + RUN:512 * j + BLK]).then_inc(S.cp, 1)
+                copy(T.r[:, place + RUN:place + BLK], ps[:, 512 * j:512 * j + RUN]).then_inc(S.cp, 1)
+
+    for w in orders["V"]:
+        do("V", vec, w)
+    for w in orders["S"]:
+        do("S", act, w)
+
+    for w in orders["T"]:
+        if len(w) == 1:
+            j = wjob.index(w)
+            buf, lo, n = window[w]
+            wait("T", ten, "qw", *needs[w])
+            for i in range(4):
+                if j >= 2:
+                    wait("T", ten, *relus(wjob[j - 2], str(i), ("", "F", "G")))
+                ten.matmul_mx(T[bank[w]][:, 512 * i:512 * i + n], T.wq[:, 128 * i:128 * i + 128], T.wqs[:, 128 * i:128 * i + 128],
+                              T[buf][:, lo:lo + n], T[buf + "s"][:, lo:lo + n], True, True).then_inc(S["m%s%d" % (w, i)], 1)
         else:
-            vec.quantize_mx(T["in%d" % p][:, pair:pair + BLK], T["ins%d" % p][:, pair:pair + BLK], src).then_inc(S["q%dG" % p], 1)
+            j = vjob.index(w)
+            wait("T", ten, "qv", *relus(wjob[-2], str(j), ("", "F", "G")))
+            if w[1] == "N":
+                wait("T", ten, "q%sG" % w[0])
+            wait("T", ten, "h" + w)
+            lo = local_lo if w[1] == "N" else far_lo
+            ten.matmul_mx(T[vbank][:, 512 * j:512 * j + BLK], T.vq[:], T.vqs[:],
+                          T["in" + w[0]][:, lo:lo + BLK], T["ins" + w[0]][:, lo:lo + BLK], True, True).then_inc(S["v" + w], 1)
 
-    def far_place(d):
-        return (0 if far.index(d) == 0 else 240) + RUN * (1 - idx)
+    def view(buf, lo, n, kind):
+        if kind == "c":
+            return T[buf][:, lo:lo + n].bitcast(dt.uint8)
+        name = buf.rstrip("01")
+        return T[name + "s" + buf[len(name):]][:, lo:lo + n]
 
-    mate_out = pair + RUN * (1 - idx)
-
-    def far_items(p, view, src, dst, m):
-        return [(d, view("%s%d" % (dst, p), far_place(d), RUN), view("%s%d" % (src, p), RUN * j, RUN), "h%dF" % p, m[j])
-                for j, d in enumerate(far)]
-
-    def near_item(p, view, buf):
-        return (near, view("%s%d" % (buf, p), 160, RUN), view("%s%d" % (buf, p), mate_out, RUN), "h%dN" % p, NEAR)
-
-    ten.wait_ge(S.qw, 1)
-    ten.wait_ge(S.qO, 1)
-    products("O", "psp", "xq", "xqs", BLK * me)
-    ten.wait_ge(S.xn, 2 * len(ne))
-    products("N", "psq", "xin", "xins", 0)
-    for i in range(4):
-        await_bank("O", i)
-        relu(i, "psp", "h0", idx, 0, 4, "O")
-    vec.wait_ge(S.lvv, 16)
-    vec.quantize_mx(T.vq[:], T.vqs[:], T.vb[:]).then_inc(S.qv, 1)
-    for i in range(4):
-        await_bank("N", i)
-        relu(i, "psq", "h0", 1 - idx, 0, 4, "N")
-    for k in "ON":
-        vec.wait_ge(S["rv" + k], 2)
-        vec.wait_ge(S["rs" + k], 2)
-    quant(0, "F")
-    quant(0, "G")
-    g.wait_ge(S.q0F, 1)
-    g.wait_ge(S.q0G, 1)
-    fused(far_items(0, codes, "hq", "in", (LOW, HIGH)) + [near_item(0, codes, "in")])
-    fused(far_items(0, plane, "hqs", "ins", (LOW, HIGH)) + [near_item(0, plane, "ins")])
-
-    ten.wait_ge(S.xa, 2 * len(fe))
-    for k in ("rvO", "rsO"):
-        ten.wait_ge(S[k], 2)
-    products("A", "psp", "xin", "xins", BLK * (1 + idx))
-    ten.wait_ge(S.xf, 2 * len(fe))
-    for k in ("rvN", "rsN"):
-        ten.wait_ge(S[k], 2)
-    products("B", "psq", "xin", "xins", BLK * (2 - idx))
-    for i in range(4):
-        await_bank("A", i)
-        relu(i, "psp", "h1", idx, 0, 4, "A")
-    for i in range(4):
-        await_bank("B", i)
-        relu(i, "psq", "h1", 1 - idx, far_b, 2, "B")
-        if i < 2:
-            relu(i, "psq", "h1", 1 - idx, grp_b, 2, "G")
-    vec.wait_ge(S.rvA, 2)
-    vec.wait_ge(S.rsA, 2)
-    vec.wait_ge(S.rvB, 2)
-    vec.wait_ge(S.rsB, 2)
-    quant(1, "F")
-    for i in (2, 3):
-        relu(i, "psq", "h1", 1 - idx, grp_b, 2, "G")
-    vec.wait_ge(S.rvG, 2)
-    vec.wait_ge(S.rsG, 2)
-    quant(1, "G")
-    g.wait_ge(S.q1F, 1)
-    fused(far_items(1, codes, "hq", "in", (LOW, HIGH)))
-    fused(far_items(1, plane, "hqs", "ins", (LOW, HIGH)))
-    g.wait_ge(S.q1G, 1)
-    it = near_item(1, codes, "in")
-    send(*it)
-    it = near_item(1, plane, "ins")
-    send(*it)
-
-    n = [0]
-
-    def level(*calls):
-        for c in calls:
-            c.then_inc(S.ar, 1)
-            n[0] += 1
-        vec.wait_ge(S.ar, n[0])
-
-    def ts(o, i, s1, s2, op0, op1=None):
-        if op1 is None:
-            return vec.tensor_scalar(T["tmp_" + o][:], i, s1, None, op0)
-        return vec.tensor_scalar(T["tmp_" + o][:], i, s1, s2, op0, op1)
-
-    def tt(o, a, b, op):
-        return vec.tensor_tensor(T["tmp_" + o][:], T["tmp_" + a][:], T["tmp_" + b][:], op)
-
-    vec.wait_ge(S.lplt, 128)
-    q = T.tmp_q[:]
-    SH = A.arith_shift_right
-    AND = A.bitwise_and
-    level(ts("t1", T.pltb[:], 1639, None, A.mult), ts("u", T.pltb[:], 2, None, A.mult))
-    level(ts("q", T.tmp_t1[:], 16, None, SH))
-    level(ts("s", q, 2, None, SH), ts("ai", q, 1, None, AND), ts("si", q, 2, 1, SH, AND),
-          ts("hs", q, 3, None, SH), ts("ha", q, 1, 1, SH, AND))
-    level(tt("ph", "hs", "ha", A.not_equal), ts("f", T.tmp_ai[:], -160, 80, A.mult, A.add), tt("g2", "u", "si", A.add))
-    level(tt("d", "ph", "s", A.subtract), tt("g1", "f", "g2", A.add))
-    level(ts("d2", T.tmp_d[:], 320, None, A.mult))
-    level(tt("g3", "g1", "d2", A.add))
-    vec.tensor_copy(T.off2[:], T.tmp_g3[:]).then_inc(S.off2, 1)
-
-    ten.wait_ge(S.qv, 1)
-    for k in ("rvA", "rsA"):
-        ten.wait_ge(S[k], 2)
-    local_lo, far_lo = (160, 0) if idx == 0 else (80, 240)
-    for j, (p, w) in enumerate(((0, "N"), (0, "F"), (1, "N"), (1, "F"))):
-        if w == "N":
-            ten.wait_ge(S["q%dG" % p], 1)
-            ten.wait_ge(S["h%dN" % p], 2 * len(ne))
+    for ps in calls:
+        tr = []
+        for dst, obuf, olo, ibuf, ilo, n, mask, sem, ready, kind in ps:
+            wait("G", g, ready)
+            rid, pid = topo.addr(T.cores[dst], core)
+            tr.append((rid, pid, view(obuf, olo, n, kind), view(ibuf, ilo, n, kind), sem, mask))
+        if len(tr) == 1:
+            rid, pid, out, in_, sem, mask = tr[0]
+            g.remote_dma(out, in_, S[sem], S.sent, pid, rid, mask)
         else:
-            ten.wait_ge(S["h%dF" % p], 2 * len(fe))
-        lo = local_lo if w == "N" else far_lo
-        ten.matmul_mx(T.psp[:, 512 * j:512 * j + BLK], T.vq[:], T.vqs[:],
-                      T["in%d" % p][:, lo:lo + BLK], T["ins%d" % p][:, lo:lo + BLK], True, True).then_inc(S["v%d%s" % (p, w)], 1)
-        place = 320 * p + 160 * (gme if w == "N" else 1 - gme)
-        out, src = T.r[:, place:place + BLK], T.psp[:, 512 * j:512 * j + BLK]
-        if j < 3:
-            act.wait_ge(S["v%d%s" % (p, w)], 1)
-            act.activation(out, src, F.Copy).then_inc(S.cs, 1)
-        else:
-            vec.wait_ge(S["v%d%s" % (p, w)], 1)
-            vec.tensor_copy(out, src).then_inc(S.cv, 1)
+            g.remote_dma_fused([RemoteDMATransfer(dst_ids=[DstId(rid=rid, pnc=pid)], dma_engine_mask=mask, remote_sem=S[sem],
+                                                  src=in_, dst=out) for rid, pid, out, in_, sem, mask in tr], local_sem=S.sent)
 
-    H = TOK // 2
-    for q_, lo in ((vec, 0), (act, H)):
-        q_.wait_ge(S.off2, 1)
-        q_.wait_ge(S.cs, 3)
-        q_.wait_ge(S.cv, 1)
-    vec.tensor_copy(T.yb[:, :H], T.r[:].indirect(T.off2[:, :H // 16])).then_inc(S.yv, 1)
-    act.activation(T.yb[:, H:], T.r[:].indirect(T.off2[:, H // 16:]), F.Copy).then_inc(S.ys, 1)
-    syn.wait_ge(S.yv, 1)
-    syn.wait_ge(S.ys, 1)
-    syn.dma_start(T.y[:], T.yb[:]).then_inc(S.yst, 16)
-    syn.wait_ge(S.yst, 16)
-    g.wait_ge(S.sent, nsent[0])
+    n = TOK // len(yjob)
+    for j, w in enumerate(yjob):
+        wait("Y", syn, w)
+        syn.dma_start(T.y[:, n * j:n * (j + 1)], T.yb[:, n * j:n * (j + 1)]).then_inc(S.yst, 16)
+    syn.wait_ge(S.yst, 16 * len(yjob))
+    wait("G", g, "sent")

from concourse.bass import DstId, RemoteDMATransfer
from concourse.mybir import dt, AluOpType, ActivationFunctionType

N, TOK, TR = 4, 512, 40
BLK = N * TR
RUN = 2 * TR
WIN = 128
HALF = 2 * BLK + 1
C = 0.043

SCRATCH = {
    "trib": ("sbuf", [128, N * N * TR // 16], "int32"),
    "off": ("sbuf", [128, N * N * TR // 16], "uint16"),
    "xb": ("sbuf", [128, 4 * TOK], "bfloat16"),
    "xt": ("sbuf", [128, 4 * N * BLK], "bfloat16"),
    "xq": ("sbuf", [128, (N + 2) * BLK], "float8_e4m3fn_x4"),
    "xqs": ("sbuf", [128, (N + 2) * BLK], "uint8"),
    "xin": ("sbuf", [128, 2 * BLK], "float8_e4m3fn_x4"),
    "xins": ("sbuf", [128, 2 * BLK], "uint8"),
    "wb": ("sbuf", [128, 2048], "bfloat16"),
    "wq": ("sbuf", [128, 512], "float8_e4m3fn_x4"),
    "wqs": ("sbuf", [128, 512], "uint8"),
    "vb": ("sbuf", [128, 512], "bfloat16"),
    "vq": ("sbuf", [128, 128], "float8_e4m3fn_x4"),
    "vqs": ("sbuf", [128, 128], "uint8"),
    "h0": ("sbuf", [128, 8 * BLK], "bfloat16"),
    "h1": ("sbuf", [128, 8 * BLK], "bfloat16"),
    "hq0": ("sbuf", [128, BLK], "float8_e4m3fn_x4"),
    "hqs0": ("sbuf", [128, BLK], "uint8"),
    "hq1": ("sbuf", [128, BLK], "float8_e4m3fn_x4"),
    "hqs1": ("sbuf", [128, BLK], "uint8"),
    "in0": ("sbuf", [128, 5 * RUN], "float8_e4m3fn_x4"),
    "ins0": ("sbuf", [128, 5 * RUN], "uint8"),
    "in1": ("sbuf", [128, 5 * RUN], "float8_e4m3fn_x4"),
    "ins1": ("sbuf", [128, 5 * RUN], "uint8"),
    "pltb": ("sbuf", [128, TOK // 16], "int32"),
    "off2": ("sbuf", [128, TOK // 16], "uint16"),
    "r": ("sbuf", [128, 2 * HALF - 1], "float32"),
    "yb": ("sbuf", [128, TOK], "float32"),
    "psp": ("psum", [128, 2048], "float32"),
    "psq": ("psum", [128, 2048], "float32"),
}
for _n in ("u", "a", "b", "c", "d"):
    SCRATCH["tmp_" + _n] = ("sbuf", [128, TOK // 16], "int32")

SEMAPHORES = ["ltri", "lx", "lw", "lvv", "lplt", "off", "qw", "qv", "ar1", "ar2", "ar3", "off2", "cp", "y0", "y1", "yst", "sent"]
for _k in "ADNO":
    SEMAPHORES += ["g" + _k, "q" + _k]
for _k in "OANBCMK":
    SEMAPHORES += ["x" + _k]
    SEMAPHORES += ["r%s%s%s" % (_k, _q, _p) for _q in "VS" for _p in ("", "F", "G")]
    SEMAPHORES += ["m%s%d" % (_k, _i) for _i in range(4)]
SEMAPHORES += ["q0F", "q0G", "q1F", "q1G", "h0N", "h0F", "h1N", "h1F", "v0N", "v0F", "v1N", "v1F"]

OPT = dict(
    V="off gA0 gA1 qA gN0 gN3 qN gD3 qD qw gO3 qO rO1 rO3 rN1 rN3 q0F rA1 q0G rB1 rB3 q1F rC1 rC3 q1G qv plt c1F y0 y1",
    S="gA2 gA3 gN1 gN2 gD0 gD1 gD2 gO0 gO1 gO2 rO0 rO2 rN0 rN2 rA0 rA2 rA3 rB0 rB2 rC0 rC2 c0F c0N c1N y0 y1",
    G="Ac Nc As+Ns Ds Bc Cc 0Fc 0Fs 1Fc+0Nc 1Fs+0Ns 1Nc 1Ns",
    T="O N A B C 0F 0N 1N 1F",
)


def rank_program(g, core, T, topo):
    me = T.rank_of(core)
    if me is None:
        return
    S = T.sem
    vec, act, ten, syn = g.vector, g.scalar, g.tensor, g.sync
    A = AluOpType
    F = ActivationFunctionType
    orders = {k: v.split() for k, v in OPT.items()}

    def chip_ranks(c):
        return [r for r in range(N) if T.cores[r] in topo.cores_of(c)]

    grp = chip_ranks(core)
    far = [r for r in range(N) if r not in grp]
    if len(grp) != 2 or grp[0] % 2 or grp[1] != grp[0] + 1 or chip_ranks(T.cores[far[0]]) != far:
        raise ValueError("the ranks must lie in neighbouring pairs on two chips")
    idx = grp.index(me)
    near = grp[1 - idx]
    gme = grp[0] // 2
    block = {"A": far[idx], "D": far[1 - idx], "N": near, "O": me}

    fe = topo.engines(core, T.cores[far[0]])
    ne = [e for e in topo.engines(core, T.cores[near]) if e not in fe]

    def bits(es):
        return sum(1 << e for e in es)

    def halves(es):
        return bits(es[:len(es) // 2]), bits(es[len(es) // 2:])

    FULL, NEAR = bits(fe), bits(ne)

    full = {"ltri": 32, "lx": 16, "lw": 16, "lvv": 16, "lplt": 32, "off": 4, "ar1": 3, "off2": 4, "cp": 7, "y0": 2, "y1": 2}
    for k in "ADNO":
        full["g" + k] = 4
    relu_sem = {}
    for qn in "VS":
        for w in orders[qn]:
            if w[0] == "r":
                relu_sem[w] = w[:2] + qn + w[3:]
                full[relu_sem[w]] = full.get(relu_sem[w], 0) + 1
    seen = set()

    def wait(qn, q, *sems):
        for s in sems:
            if (qn, s) not in seen:
                seen.add((qn, s))
                q.wait_ge(S[s], full.get(s, 1))

    def relus(ks, banks, parts):
        return [s for w, s in relu_sem.items() if w[1] in ks and w[2] in banks and w[3:] in parts]

    syn.dma_start(T.trib[0:16, :], T.tri[:]).then_inc(S.ltri, 16)
    act.dma_start(T.trib[16:32, :], T.tri[:]).then_inc(S.ltri, 16)
    syn.dma_start(T.xb[:], T.x[:]).then_inc(S.lx, 16)
    syn.dma_start(T.wb[:], T.w[:]).then_inc(S.lw, 16)
    syn.dma_start(T.vb[:], T.vv[:]).then_inc(S.lvv, 16)
    for k in range(2):
        syn.dma_start(T.pltb[16 * k:16 * k + 16, :], T.plt[:]).then_inc(S.lplt, 16)

    far_b, grp_b = far[0], grp[0]
    pair = 3 * RUN if idx == 0 else 0
    local_lo, far_lo = (2 * RUN, 0) if idx == 0 else (RUN, 3 * RUN)

    def mine(r):
        return BLK * (1 + r)

    n_at = (N + 1) * BLK * gme

    def far_at(sender_chip):
        return {"A": BLK * sender_chip, "D": BLK * (1 - sender_chip)}

    def pieces(k):
        if k in "NMK":
            lo, n = {"N": (0, BLK), "M": (RUN * (1 - gme), RUN), "K": (RUN * gme, RUN)}[k]
            return [(near, "xq", n_at + lo, "xq", mine(near) + lo, n, NEAR, {"N": "xM"}.get(k, "x" + k), "qN")]
        if k == "A":
            return [(block[k], "xin", far_at(gme)[k], "xq", mine(block[k]), BLK, FULL, "xA", "qA")]
        if k in "DBC":
            lo, n = {"D": (0, BLK), "B": (RUN * gme, RUN), "C": (RUN * (1 - gme), RUN)}[k]
            return [(block["D"], "xin", far_at(gme)["D"] + lo, "xq", mine(block["D"]) + lo, n, FULL, {"D": "xB"}.get(k, "x" + k), "qD")]
        p = k[0]
        if k[1] == "N":
            return [(near, "in" + p, 2 * RUN, "in" + p, pair + RUN * (1 - idx), RUN, NEAR, "h" + k, "q%sG" % p)]
        return [(d, "in" + p, 3 * RUN * j + RUN * idx, "hq" + p, RUN * j, RUN, FULL, "h" + k, "q" + k) for j, d in enumerate(far)]

    calls = []
    for call in orders["G"]:
        ps = [list(p) + [it[-1]] for it in call.split("+") for p in pieces(it[:-1])]
        for mask, es in ((FULL, fe), (NEAR, ne)):
            two = [p for p in ps if p[6] == mask]
            if len(two) == 2:
                two[0][6], two[1][6] = halves(es)
        calls.append(ps)
        for p in ps:
            for k in (p[7], "sent"):
                full[k] = full.get(k, 0) + bin(p[6]).count("1")
    at = far_at(1 - gme)
    skip = (WIN - RUN) * gme
    first, second = RUN * (1 - gme) - skip, RUN * gme - skip
    window = {"O": ("xq", mine(me), BLK), "A": ("xin", at["A"], BLK), "N": ("xq", n_at, BLK),
              "M": ("xq", n_at + first, WIN), "K": ("xq", n_at + second, WIN),
              "B": ("xin", at["D"] + first, WIN), "C": ("xin", at["D"] + second, WIN)}
    needs = {"O": ["qO"], "N": ["xM"], "A": ["xA"], "M": ["qN", "qO", "xM"], "K": ["xM", "xK"], "B": ["xA", "xB"], "C": ["xB", "xC"]}

    wjob = [w for w in orders["T"] if len(w) == 1]
    vjob = [w for w in orders["T"] if len(w) == 2]
    yjob = [w for w in orders["V"] if w[0] == "y"]
    bank = {w: ("psp", "psq")[j % 2] for j, w in enumerate(wjob)}
    vbank = bank[wjob[-2]]
    KO = BLK // 16

    def do(qn, q, w):
        def copy(out, src):
            return q.tensor_copy(out, src) if qn == "V" else q.activation(out, src, F.Copy)

        if w == "off":
            wait(qn, q, "ltri")
            for p in range(0, 128, 32):
                q.tensor_scalar(T.off[p:p + 32, :], T.trib[0:32, :], 4, 0, A.mult, A.max).then_inc(S.off, 1)
        elif w == "qw":
            wait(qn, q, "lw")
            q.quantize_mx(T.wq[:], T.wqs[:], T.wb[:]).then_inc(S.qw, 1)
        elif w == "qv":
            wait(qn, q, "lvv")
            q.quantize_mx(T.vq[:], T.vqs[:], T.vb[:]).then_inc(S.qv, 1)
        elif w == "plt":
            e = T.pltb[0:32, :]
            t = {k: T["tmp_" + k][0:32, :] for k in "uabcd"}
            wait(qn, q, "lplt")
            q.memset(T.r[:, HALF - 1:HALF], 0.0).then_inc(S.cp, 1)
            q.tensor_scalar(t["u"], e, 2, None, A.mult).then_inc(S.ar1, 1)
            q.tensor_scalar(t["a"], e, BLK, 2 - HALF, A.is_ge, A.mult).then_inc(S.ar1, 1)
            q.tensor_scalar(t["b"], e, 3 * BLK, 2 - HALF, A.is_ge, A.mult).then_inc(S.ar1, 1)
            wait(qn, q, "ar1")
            q.tensor_tensor(t["c"], t["u"], t["a"], A.add).then_inc(S.ar2, 1)
            wait(qn, q, "ar2")
            q.tensor_tensor(t["d"], t["c"], t["b"], A.add).then_inc(S.ar3, 1)
            wait(qn, q, "ar3")
            for p in range(0, 128, 32):
                q.tensor_copy(T.off2[p:p + 32, :], t["d"]).then_inc(S.off2, 1)
        elif w[0] == "y":
            n = TOK // (2 * len(yjob))
            lo = n * (2 * int(w[1]) + (qn == "S"))
            wait(qn, q, "off2", "cp")
            copy(T.yb[:, lo:lo + n], T.r[:].indirect(T.off2[:, lo // 16:(lo + n) // 16])).then_inc(S[w], 1)
        elif w[0] == "g":
            a, t = block[w[1]], int(w[2])
            wait(qn, q, "off", "lx")
            copy(T.xt[:, 4 * BLK * a + t:4 * BLK * (a + 1):4],
                 T.xb[:, t:4 * TOK].indirect(T.off[:, KO * a:KO * a + KO])).then_inc(S["g" + w[1]], 1)
        elif w[0] == "q" and len(w) == 2:
            a = block[w[1]]
            wait(qn, q, "g" + w[1])
            q.quantize_mx(T.xq[:, mine(a):mine(a) + BLK], T.xqs[:, mine(a):mine(a) + BLK],
                          T.xt[:, 4 * BLK * a:4 * BLK * (a + 1)]).then_inc(S[w], 1)
        elif w[0] == "r":
            k, i = w[1], int(w[2])
            part = "F" if k in "MB" else "G" if k in "KC" else w[3:]
            b0, nb = {"": (0, 4), "F": (far_b, 2), "G": (grp_b, 2)}[part]
            si = idx if k in "OA" else 1 - idx
            lo = 512 * i + (TR * b0 if k in "OAN" else skip)
            src = T[bank[k]][:, lo:lo + TR * nb]
            out = T["h0" if k in "ONMK" else "h1"][:, 8 * TR * b0 + 4 * si + i:8 * TR * (b0 + nb):8]
            wait(qn, q, "m%s%d" % (k, i))
            if qn == "V":
                q.tensor_scalar(out, src, 0.0, C, A.max, A.mult).then_inc(S[relu_sem[w]], 1)
            else:
                q.activation(out, src, F.Relu, scale=C).then_inc(S[relu_sem[w]], 1)
        elif w[0] == "q":
            p, part = w[1], w[2]
            b0 = far_b if part == "F" else grp_b
            src = T["h" + p][:, 8 * TR * b0:8 * TR * (b0 + 2)]
            wait(qn, q, *relus({"0F": "ONM", "0G": "ONK", "1F": "AB", "1G": "AC"}[w[1:]], "0123", ("", part)))
            if part == "F":
                q.quantize_mx(T["hq" + p][:], T["hqs" + p][:], src).then_inc(S[w], 1)
            else:
                q.quantize_mx(T["in" + p][:, pair:pair + BLK], T["ins" + p][:, pair:pair + BLK], src).then_inc(S[w], 1)
        elif w[0] == "c":
            j = vjob.index(w[1:])
            ga = gme if w[2] == "N" else 1 - gme
            gs = ga if w[1] == "0" else 1 - ga
            place = HALF * gs + BLK * ga
            ps = T[vbank]
            wait(qn, q, "v" + w[1:])
            if w[2] == "F":
                copy(T.r[:, place:place + BLK], ps[:, 512 * j:512 * j + BLK]).then_inc(S.cp, 1)
            else:
                copy(T.r[:, place:place + RUN], ps[:, 512 * j + RUN:512 * j + BLK]).then_inc(S.cp, 1)
                copy(T.r[:, place + RUN:place + BLK], ps[:, 512 * j:512 * j + RUN]).then_inc(S.cp, 1)

    for w in orders["V"]:
        do("V", vec, w)
    for w in orders["S"]:
        do("S", act, w)

    for w in orders["T"]:
        if len(w) == 1:
            j = wjob.index(w)
            buf, lo, n = window[w]
            wait("T", ten, "qw", *needs[w])
            for i in range(4):
                if j >= 2:
                    wait("T", ten, *relus(wjob[j - 2], str(i), ("", "F", "G")))
                ten.matmul_mx(T[bank[w]][:, 512 * i:512 * i + n], T.wq[:, 128 * i:128 * i + 128], T.wqs[:, 128 * i:128 * i + 128],
                              T[buf][:, lo:lo + n], T[buf + "s"][:, lo:lo + n], True, True).then_inc(S["m%s%d" % (w, i)], 1)
        else:
            j = vjob.index(w)
            wait("T", ten, "qv", *relus(wjob[-2], str(j), ("", "F", "G")))
            if w[1] == "N":
                wait("T", ten, "q%sG" % w[0])
            wait("T", ten, "h" + w)
            lo = local_lo if w[1] == "N" else far_lo
            ten.matmul_mx(T[vbank][:, 512 * j:512 * j + BLK], T.vq[:], T.vqs[:],
                          T["in" + w[0]][:, lo:lo + BLK], T["ins" + w[0]][:, lo:lo + BLK], True, True).then_inc(S["v" + w], 1)

    def view(buf, lo, n, kind):
        if kind == "c":
            return T[buf][:, lo:lo + n].bitcast(dt.uint8)
        name = buf.rstrip("01")
        return T[name + "s" + buf[len(name):]][:, lo:lo + n]

    for ps in calls:
        tr = []
        for dst, obuf, olo, ibuf, ilo, n, mask, sem, ready, kind in ps:
            wait("G", g, ready)
            rid, pid = topo.addr(T.cores[dst], core)
            tr.append((rid, pid, view(obuf, olo, n, kind), view(ibuf, ilo, n, kind), sem, mask))
        if len(tr) == 1:
            rid, pid, out, in_, sem, mask = tr[0]
            g.remote_dma(out, in_, S[sem], S.sent, pid, rid, mask)
        else:
            g.remote_dma_fused([RemoteDMATransfer(dst_ids=[DstId(rid=rid, pnc=pid)], dma_engine_mask=mask, remote_sem=S[sem],
                                                  src=in_, dst=out) for rid, pid, out, in_, sem, mask in tr], local_sem=S.sent)

    n = TOK // len(yjob)
    for j, w in enumerate(yjob):
        wait("Y", syn, w)
        syn.dma_start(T.y[:, n * j:n * (j + 1)], T.yb[:, n * j:n * (j + 1)]).then_inc(S.yst, 16)
    syn.wait_ge(S.yst, 16 * len(yjob))
    wait("G", g, "sent")
